import numpy as np, ml_dtypes
CORES = [34,162,290,418,42,426]
N = 6
import mx_ref
NC, HD, G = 128, 1, 4
C, DEC = np.float32(0.023), np.float32(0.8)
BF = ml_dtypes.bfloat16
def cut(t, i, w=512):
    return t[:, w * i:w * i + w]
def tile(rs):
    return np.stack(rs, axis=2).reshape(128, -1).astype(BF)
def layer(w, X):
    out = []
    for i in range(G):
        for t in range(len(X)):
            p = mx_ref.matmul(mx_ref.quantize(cut(w, len(X) * i + t)), X[t])
            z = p if t == 0 else z + p
        out.append(z)
    return out
def pick(b):
    s = np.zeros((128, 128, 4), np.float32)
    s[np.arange(128), np.arange(128), b] = 1.0
    return mx_ref.quantize(s.reshape(128, 512).astype(BF))
def setup_inputs(rng):
    def f(*shape):
        return mx_ref.flush((rng.standard_normal(shape, dtype=np.float32) * np.exp2(rng.integers(-2, 3, shape[:-1] + (1,)))).astype(BF))
    return {"k": f(N, 128, HD * 4 * 512), "v": f(N, 128, HD * 512), "q": f(N, 128, HD * 4 * NC)}
def setup_inputs_blocks(rng):
    d = setup_inputs(rng)
    for k in ("k", "v", "q"): d[k] = mx_ref.spread(d[k], rng, 4)
    return d
def setup_inputs_wide(rng):
    d = setup_inputs(rng)
    for k in ("k", "v", "q"): d[k] = mx_ref.flush((d[k].astype(np.float32) * np.exp2(rng.integers(-4, 5, (N, 1, 1))).astype(np.float32)).astype(BF))
    return d
def setup_inputs_zeros(rng):
    d = setup_inputs(rng); v = d["v"].reshape(N, 128, -1, 4).copy()
    v[np.broadcast_to((rng.random((N, 1, v.shape[2], 1)) < 0.33), v.shape)] = 0
    d["v"] = v.reshape(d["v"].shape)
    return d
def reference(k, v, q):
    S = [pick(t) for t in range(4)]
    y = np.zeros((N, 128, HD * NC), np.float32)
    for a in range(HD):
        for r in range(N):
            R = [z * C for z in layer(cut(k[r], a, 4 * 512), [mx_ref.quantize(cut(v[r], a))])]
            if r > 0: R = [R[t] + mx_ref.matmul(S[t], s) * DEC for t in range(4)]
            s = mx_ref.quantize(tile(R))
            y[r][:, NC * a:NC * a + NC] = mx_ref.matmul(s, mx_ref.quantize(cut(q[r], a, 4 * NC)))
    return {"y": y}

@@ -1,0 +1,125 @@
+from concourse.mybir import dt, AluOpType, ActivationFunctionType
+
+NB = 4
+W = 128
+E = 4 * W
+BANK = 512
+C = 0.023
+DEC = 0.8
+
+CODES = "float8_e4m3fn_x4"
+SCRATCH = {
+    "kt": ("sbuf", [128, NB * E], "bfloat16"),
+    "vt": ("sbuf", [128, E], "bfloat16"),
+    "qt": ("sbuf", [128, E], "bfloat16"),
+    "kc": ("sbuf", [128, NB * W], CODES), "kp": ("sbuf", [128, NB * W], "uint8"),
+    "vc": ("sbuf", [128, W], CODES), "vp": ("sbuf", [128, W], "uint8"),
+    "qc": ("sbuf", [128, W], CODES), "qp": ("sbuf", [128, W], "uint8"),
+    "e": ("sbuf", [128, E + 4], "bfloat16"),
+    "sc": ("sbuf", [128, NB * W], CODES), "sp": ("sbuf", [128, NB * W], "uint8"),
+    "rc": ("sbuf", [128, W], CODES), "rp": ("sbuf", [128, W], "uint8"),
+    "zs": ("sbuf", [128, NB * W], "float32"),
+    "ds": ("sbuf", [128, NB * W], "float32"),
+    "tile": ("sbuf", [128, E], "bfloat16"),
+    "tc": ("sbuf", [128, W], CODES), "tp": ("sbuf", [128, W], "uint8"),
+    "ys": ("sbuf", [128, W], "float32"),
+    "zb": ("psum", [128, NB * BANK], "float32"),
+    "db": ("psum", [128, NB * BANK], "float32"),
+}
+SEMAPHORES = (["vin", "kin", "qin", "vq", "qq", "ones", "esel", "sq", "zsc", "til", "st", "ymm", "ycp", "yout", "arr", "sent"]
+              + ["%s%d" % (s, b) for s in ("kq", "zm", "dm", "dsc") for b in range(NB)])
+
+
+def rank_program(g, core, T, topo):
+    rank = T.rank_of(core)
+    if rank is None:
+        return
+    n = len(T.cores)
+    first, last = rank == 0, rank == n - 1
+    s = T.sem
+    copy = ActivationFunctionType.Copy
+
+    def cut(b, w=W):
+        return slice(w * b, w * b + w)
+
+    def bank(b):
+        return slice(BANK * b, BANK * b + W)
+
+    def strip(b):
+        return slice(b, E, NB)
+
+    def engines(src, dst):
+        return bin(topo.mask(src, dst)).count("1")
+
+    g.sync.dma_start(T.vt[:], T.v[:]).then_inc(s.vin, 16)
+    g.sync.dma_start(T.kt[:], T.k[:]).then_inc(s.kin, 16)
+    if not first:
+        g.sync.dma_start(T.qt[:], T.q[:]).then_inc(s.qin, 16)
+
+    if not first:
+        g.vector.memset(T.e[:], 1.0).then_inc(s.ones, 1)
+        g.wait_ge(s.ones, 1)
+        g.affine_select(T.e[:], T.e[:], [[-1, E + 4]], AluOpType.is_equal, 0.0, NB - 1, NB).then_inc(s.esel, 1)
+
+    g.vector.wait_ge(s.vin, 16)
+    g.vector.quantize_mx(T.vc[:, 0:W], T.vp[:, 0:W], T.vt[:, 0:E]).then_inc(s.vq, 1)
+    g.vector.wait_ge(s.kin, 16)
+    g.tensor.wait_ge(s.vq, 1)
+    for b in range(NB):
+        g.vector.quantize_mx(T.kc[:, cut(b)], T.kp[:, cut(b)], T.kt[:, cut(b, E)]).then_inc(s["kq%d" % b], 1)
+        g.tensor.wait_ge(s["kq%d" % b], 1)
+        g.tensor.matmul_mx(T.zb[:, bank(b)], T.kc[:, cut(b)], T.kp[:, cut(b)], T.vc[:, 0:W], T.vp[:, 0:W], True, True).then_inc(s["zm%d" % b], 1)
+
+    if first:
+        for b in range(NB - 1):
+            g.scalar.wait_ge(s["zm%d" % b], 1)
+            g.scalar.activation(T.tile[:, strip(b)], T.zb[:, bank(b)], copy, scale=C).then_inc(s.zsc, 1)
+        b = NB - 1
+        g.vector.wait_ge(s["zm%d" % b], 1)
+        g.vector.tensor_scalar(T.tile[:, strip(b)], T.zb[:, bank(b)], C, None, AluOpType.mult).then_inc(s.til, 1)
+        g.vector.wait_ge(s.zsc, NB - 1)
+        g.vector.wait_ge(s.til, 1)
+    else:
+        g.vector.wait_ge(s.esel, 1)
+        for b in range(NB):
+            g.vector.quantize_mx(T.sc[:, cut(b)], T.sp[:, cut(b)], T.e[:, NB - 1 - b:NB - 1 - b + E]).then_inc(s.sq, 1)
+        g.vector.wait_ge(s.qin, 16)
+        g.vector.quantize_mx(T.qc[:, 0:W], T.qp[:, 0:W], T.qt[:, 0:E]).then_inc(s.qq, 1)
+        for b in range(NB):
+            g.scalar.wait_ge(s["zm%d" % b], 1)
+            g.scalar.activation(T.zs[:, cut(b)], T.zb[:, bank(b)], copy, scale=C).then_inc(s.zsc, 1)
+        g.tensor.wait_ge(s.sq, NB)
+        g.tensor.wait_ge(s.qq, 1)
+        g.tensor.wait_ge(s.arr, 2 * engines(T.cores[rank - 1], core))
+        g.vector.wait_ge(s.zsc, NB)
+        for b in range(NB):
+            g.tensor.matmul_mx(T.db[:, bank(b)], T.sc[:, cut(b)], T.sp[:, cut(b)], T.rc[:, 0:W], T.rp[:, 0:W], True, True).then_inc(s["dm%d" % b], 1)
+            g.scalar.wait_ge(s["dm%d" % b], 1)
+            g.scalar.activation(T.ds[:, cut(b)], T.db[:, bank(b)], copy, scale=DEC).then_inc(s["dsc%d" % b], 1)
+            g.vector.wait_ge(s["dsc%d" % b], 1)
+            g.vector.tensor_tensor(T.tile[:, strip(b)], T.zs[:, cut(b)], T.ds[:, cut(b)], AluOpType.add).then_inc(s.til, 1)
+        g.vector.wait_ge(s.til, NB)
+
+    g.vector.quantize_mx(T.tc[:, 0:W], T.tp[:, 0:W], T.tile[:, 0:E]).then_inc(s.st, 1)
+
+    if not last:
+        dst = T.cores[rank + 1]
+        rid, pid = topo.addr(dst, core)
+        mask = topo.mask(core, dst)
+        g.wait_ge(s.st, 1)
+        g.remote_dma(T.rc[:, 0:W].bitcast(dt.uint8), T.tc[:, 0:W].bitcast(dt.uint8), s.arr, s.sent, pid, rid, mask)
+        g.remote_dma(T.rp[:, 0:W], T.tp[:, 0:W], s.arr, s.sent, pid, rid, mask)
+        g.sync.wait_ge(s.sent, 2 * engines(core, dst))
+        if first:
+            g.sync.dma_start(T.qt[:], T.q[:]).then_inc(s.qin, 16)
+            g.vector.wait_ge(s.qin, 16)
+            g.vector.quantize_mx(T.qc[:, 0:W], T.qp[:, 0:W], T.qt[:, 0:E]).then_inc(s.qq, 1)
+            g.tensor.wait_ge(s.qq, 1)
+
+    g.tensor.wait_ge(s.st, 1)
+    g.tensor.matmul_mx(T.zb[:, bank(0)], T.tc[:, 0:W], T.tp[:, 0:W], T.qc[:, 0:W], T.qp[:, 0:W], True, True).then_inc(s.ymm, 1)
+    g.vector.wait_ge(s.ymm, 1)
+    g.vector.tensor_copy(T.ys[:], T.zb[:, bank(0)]).then_inc(s.ycp, 1)
+    g.sync.wait_ge(s.ycp, 1)
+    g.sync.dma_start(T.y[:], T.ys[:]).then_inc(s.yout, 16)
+    g.sync.wait_ge(s.yout, 16)

@@ -4,6 +4,7 @@ NB = 4
 W = 128
 E = 4 * W
 BANK = 512
+HEAD = 32
 C = 0.023
 DEC = 0.8
 
@@ -15,7 +16,9 @@ SCRATCH = {
     "kc": ("sbuf", [128, NB * W], CODES), "kp": ("sbuf", [128, NB * W], "uint8"),
     "vc": ("sbuf", [128, W], CODES), "vp": ("sbuf", [128, W], "uint8"),
     "qc": ("sbuf", [128, W], CODES), "qp": ("sbuf", [128, W], "uint8"),
-    "e": ("sbuf", [128, E + 4], "bfloat16"),
+    "h": ("sbuf", [128, E], "bfloat16"),
+    "hc": ("sbuf", [128, W], CODES), "hp": ("sbuf", [128, W], "uint8"),
+    "f": ("sbuf", [128, 2 * E], "bfloat16"),
     "sc": ("sbuf", [128, NB * W], CODES), "sp": ("sbuf", [128, NB * W], "uint8"),
     "rc": ("sbuf", [128, W], CODES), "rp": ("sbuf", [128, W], "uint8"),
     "zs": ("sbuf", [128, NB * W], "float32"),
@@ -26,8 +29,10 @@ SCRATCH = {
     "zb": ("psum", [128, NB * BANK], "float32"),
     "db": ("psum", [128, NB * BANK], "float32"),
 }
-SEMAPHORES = (["vin", "kin", "qin", "vq", "qq", "ones", "esel", "sq", "zsc", "til", "st", "ymm", "ycp", "yout", "arr", "sent"]
-              + ["%s%d" % (s, b) for s in ("kq", "zm", "dm", "dsc") for b in range(NB)])
+SEMAPHORES = (["vin", "kin0", "kin1", "qin", "vq", "qq", "hone", "hzero", "hsel", "hq", "harr", "hsent", "fone", "fsel", "sq", "zsc",
+               "til", "st", "ymm", "ycp", "yout", "arr", "sent"]
+              + ["%s%d" % (s, b) for s in ("kq", "zm", "dm") for b in range(NB)]
+              + ["dsc%d" % i for i in range(NB + 1)])
 
 
 def rank_program(g, core, T, topo):
@@ -42,30 +47,51 @@ def rank_program(g, core, T, topo):
     def cut(b, w=W):
         return slice(w * b, w * b + w)
 
-    def bank(b):
-        return slice(BANK * b, BANK * b + W)
-
-    def strip(b):
-        return slice(b, E, NB)
-
     def engines(src, dst):
         return bin(topo.mask(src, dst)).count("1")
 
-    g.sync.dma_start(T.vt[:], T.v[:]).then_inc(s.vin, 16)
-    g.sync.dma_start(T.kt[:], T.k[:]).then_inc(s.kin, 16)
-    if not first:
-        g.sync.dma_start(T.qt[:], T.q[:]).then_inc(s.qin, 16)
+    def bank(b, lo=0, hi=W):
+        return slice(BANK * b + lo, BANK * b + hi)
 
+    def strip(b, lo=0, hi=W):
+        return slice(b + NB * lo, NB * hi, NB)
+
+    if not last:
+        dst = T.cores[rank + 1]
+        rid, pid = topo.addr(dst, core)
+        mask = topo.mask(core, dst)
+
+    g.scalar.dma_start(T.vt[:], T.v[:]).then_inc(s.vin, 16)
+    g.sync.dma_start(T.kt[:, 0:(NB - 1) * E], T.k[:, 0:(NB - 1) * E]).then_inc(s.kin0, 16)
+    g.sync.dma_start(T.kt[:, cut(NB - 1, E)], T.k[:, cut(NB - 1, E)]).then_inc(s.kin1, 16)
     if not first:
-        g.vector.memset(T.e[:], 1.0).then_inc(s.ones, 1)
-        g.wait_ge(s.ones, 1)
-        g.affine_select(T.e[:], T.e[:], [[-1, E + 4]], AluOpType.is_equal, 0.0, NB - 1, NB).then_inc(s.esel, 1)
+        g.scalar.dma_start(T.qt[:], T.q[:]).then_inc(s.qin, 16)
+
+    hw = NB * HEAD
+    if not last:
+        g.vector.memset(T.h[:, 0:hw], 1.0).then_inc(s.hone, 1)
+        g.wait_ge(s.hone, 1)
+        g.affine_select(T.h[:, 0:hw], T.h[:, 0:hw], [[-1, hw]], AluOpType.is_equal, 0.0, 0, NB).then_inc(s.hsel, 1)
+        g.vector.memset(T.h[:, hw:E], 0.0).then_inc(s.hzero, 1)
+    if not first:
+        g.vector.memset(T.f[:], 1.0).then_inc(s.fone, 1)
+        g.wait_ge(s.fone, 1)
+        g.affine_select(T.f[:], T.f[:], [[1, 2], [-1, E]], AluOpType.is_equal, 0.0, 0, NB).then_inc(s.fsel, 1)
+    if not last:
+        g.vector.wait_ge(s.hzero, 1)
+        g.vector.wait_ge(s.hsel, 1)
+        g.vector.quantize_mx(T.hc[:, 0:W], T.hp[:, 0:W], T.h[:, 0:E]).then_inc(s.hq, 1)
+        g.wait_ge(s.hq, 1)
+        g.remote_dma(T.sc[:, 0:HEAD].bitcast(dt.uint8), T.hc[:, 0:HEAD].bitcast(dt.uint8), s.harr, s.hsent, pid, rid, mask)
+        g.remote_dma(T.sp[:, 0:HEAD], T.hp[:, 0:HEAD], s.harr, s.hsent, pid, rid, mask)
 
     g.vector.wait_ge(s.vin, 16)
     g.vector.quantize_mx(T.vc[:, 0:W], T.vp[:, 0:W], T.vt[:, 0:E]).then_inc(s.vq, 1)
-    g.vector.wait_ge(s.kin, 16)
+    g.vector.wait_ge(s.kin0, 16)
     g.tensor.wait_ge(s.vq, 1)
     for b in range(NB):
+        if b == NB - 1:
+            g.vector.wait_ge(s.kin1, 16)
         g.vector.quantize_mx(T.kc[:, cut(b)], T.kp[:, cut(b)], T.kt[:, cut(b, E)]).then_inc(s["kq%d" % b], 1)
         g.tensor.wait_ge(s["kq%d" % b], 1)
         g.tensor.matmul_mx(T.zb[:, bank(b)], T.kc[:, cut(b)], T.kp[:, cut(b)], T.vc[:, 0:W], T.vp[:, 0:W], True, True).then_inc(s["zm%d" % b], 1)
@@ -80,35 +106,40 @@ def rank_program(g, core, T, topo):
         g.vector.wait_ge(s.zsc, NB - 1)
         g.vector.wait_ge(s.til, 1)
     else:
-        g.vector.wait_ge(s.esel, 1)
-        for b in range(NB):
-            g.vector.quantize_mx(T.sc[:, cut(b)], T.sp[:, cut(b)], T.e[:, NB - 1 - b:NB - 1 - b + E]).then_inc(s.sq, 1)
+        g.vector.wait_ge(s.fsel, 1)
+        g.vector.quantize_mx(T.sc[:, HEAD:2 * W], T.sp[:, HEAD:2 * W], T.f[:, hw:2 * E]).then_inc(s.sq, 1)
+        for b in range(2, NB):
+            g.vector.quantize_mx(T.sc[:, cut(b)], T.sp[:, cut(b)], T.f[:, E + 1 - b:2 * E + 1 - b]).then_inc(s.sq, 1)
         g.vector.wait_ge(s.qin, 16)
         g.vector.quantize_mx(T.qc[:, 0:W], T.qp[:, 0:W], T.qt[:, 0:E]).then_inc(s.qq, 1)
         for b in range(NB):
             g.scalar.wait_ge(s["zm%d" % b], 1)
             g.scalar.activation(T.zs[:, cut(b)], T.zb[:, bank(b)], copy, scale=C).then_inc(s.zsc, 1)
-        g.tensor.wait_ge(s.sq, NB)
+        g.tensor.wait_ge(s.sq, NB - 1)
         g.tensor.wait_ge(s.qq, 1)
-        g.tensor.wait_ge(s.arr, 2 * engines(T.cores[rank - 1], core))
+        got = 2 * engines(T.cores[rank - 1], core)
+        g.tensor.wait_ge(s.harr, got)
+        g.tensor.wait_ge(s.arr, got)
         g.vector.wait_ge(s.zsc, NB)
         for b in range(NB):
             g.tensor.matmul_mx(T.db[:, bank(b)], T.sc[:, cut(b)], T.sp[:, cut(b)], T.rc[:, 0:W], T.rp[:, 0:W], True, True).then_inc(s["dm%d" % b], 1)
-            g.scalar.wait_ge(s["dm%d" % b], 1)
-            g.scalar.activation(T.ds[:, cut(b)], T.db[:, bank(b)], copy, scale=DEC).then_inc(s["dsc%d" % b], 1)
-            g.vector.wait_ge(s["dsc%d" % b], 1)
-            g.vector.tensor_tensor(T.tile[:, strip(b)], T.zs[:, cut(b)], T.ds[:, cut(b)], AluOpType.add).then_inc(s.til, 1)
-        g.vector.wait_ge(s.til, NB)
+        pieces = [(0, 0, W // 2), (0, W // 2, W)] + [(b, 0, W) for b in range(1, NB)]
+        for i, (b, lo, hi) in enumerate(pieces):
+            if lo == 0:
+                g.scalar.wait_ge(s["dm%d" % b], 1)
+            c = slice(W * b + lo, W * b + hi)
+            g.scalar.activation(T.ds[:, c], T.db[:, bank(b, lo, hi)], copy, scale=DEC).then_inc(s["dsc%d" % i], 1)
+            g.vector.wait_ge(s["dsc%d" % i], 1)
+            g.vector.tensor_tensor(T.tile[:, strip(b, lo, hi)], T.zs[:, c], T.ds[:, c], AluOpType.add).then_inc(s.til, 1)
+        g.vector.wait_ge(s.til, len(pieces))
 
     g.vector.quantize_mx(T.tc[:, 0:W], T.tp[:, 0:W], T.tile[:, 0:E]).then_inc(s.st, 1)
 
     if not last:
-        dst = T.cores[rank + 1]
-        rid, pid = topo.addr(dst, core)
-        mask = topo.mask(core, dst)
         g.wait_ge(s.st, 1)
         g.remote_dma(T.rc[:, 0:W].bitcast(dt.uint8), T.tc[:, 0:W].bitcast(dt.uint8), s.arr, s.sent, pid, rid, mask)
         g.remote_dma(T.rp[:, 0:W], T.tp[:, 0:W], s.arr, s.sent, pid, rid, mask)
+        g.wait_ge(s.hsent, 2 * engines(core, dst))
         g.sync.wait_ge(s.sent, 2 * engines(core, dst))
         if first:
             g.sync.dma_start(T.qt[:], T.q[:]).then_inc(s.qin, 16)

from concourse.mybir import dt, AluOpType, ActivationFunctionType

NB = 4
W = 128
E = 4 * W
BANK = 512
HEAD = 32
C = 0.023
DEC = 0.8

CODES = "float8_e4m3fn_x4"
SCRATCH = {
    "kt": ("sbuf", [128, NB * E], "bfloat16"),
    "vt": ("sbuf", [128, E], "bfloat16"),
    "qt": ("sbuf", [128, E], "bfloat16"),
    "kc": ("sbuf", [128, NB * W], CODES), "kp": ("sbuf", [128, NB * W], "uint8"),
    "vc": ("sbuf", [128, W], CODES), "vp": ("sbuf", [128, W], "uint8"),
    "qc": ("sbuf", [128, W], CODES), "qp": ("sbuf", [128, W], "uint8"),
    "h": ("sbuf", [128, E], "bfloat16"),
    "hc": ("sbuf", [128, W], CODES), "hp": ("sbuf", [128, W], "uint8"),
    "f": ("sbuf", [128, 2 * E], "bfloat16"),
    "sc": ("sbuf", [128, NB * W], CODES), "sp": ("sbuf", [128, NB * W], "uint8"),
    "rc": ("sbuf", [128, W], CODES), "rp": ("sbuf", [128, W], "uint8"),
    "zs": ("sbuf", [128, NB * W], "float32"),
    "ds": ("sbuf", [128, NB * W], "float32"),
    "tile": ("sbuf", [128, E], "bfloat16"),
    "tc": ("sbuf", [128, W], CODES), "tp": ("sbuf", [128, W], "uint8"),
    "ys": ("sbuf", [128, W], "float32"),
    "zb": ("psum", [128, NB * BANK], "float32"),
    "db": ("psum", [128, NB * BANK], "float32"),
}
SEMAPHORES = (["vin", "kin0", "kin1", "qin", "vq", "qq", "hone", "hzero", "hsel", "hq", "harr", "hsent", "fone", "fsel", "sq", "zsc",
               "til", "st", "ymm", "ycp", "yout", "arr", "sent"]
              + ["%s%d" % (s, b) for s in ("kq", "zm", "dm") for b in range(NB)]
              + ["dsc%d" % i for i in range(NB + 1)])


def rank_program(g, core, T, topo):
    rank = T.rank_of(core)
    if rank is None:
        return
    n = len(T.cores)
    first, last = rank == 0, rank == n - 1
    s = T.sem
    copy = ActivationFunctionType.Copy

    def cut(b, w=W):
        return slice(w * b, w * b + w)

    def engines(src, dst):
        return bin(topo.mask(src, dst)).count("1")

    def bank(b, lo=0, hi=W):
        return slice(BANK * b + lo, BANK * b + hi)

    def strip(b, lo=0, hi=W):
        return slice(b + NB * lo, NB * hi, NB)

    if not last:
        dst = T.cores[rank + 1]
        rid, pid = topo.addr(dst, core)
        mask = topo.mask(core, dst)

    g.scalar.dma_start(T.vt[:], T.v[:]).then_inc(s.vin, 16)
    g.sync.dma_start(T.kt[:, 0:(NB - 1) * E], T.k[:, 0:(NB - 1) * E]).then_inc(s.kin0, 16)
    g.sync.dma_start(T.kt[:, cut(NB - 1, E)], T.k[:, cut(NB - 1, E)]).then_inc(s.kin1, 16)
    if not first:
        g.scalar.dma_start(T.qt[:], T.q[:]).then_inc(s.qin, 16)

    hw = NB * HEAD
    if not last:
        g.vector.memset(T.h[:, 0:hw], 1.0).then_inc(s.hone, 1)
        g.wait_ge(s.hone, 1)
        g.affine_select(T.h[:, 0:hw], T.h[:, 0:hw], [[-1, hw]], AluOpType.is_equal, 0.0, 0, NB).then_inc(s.hsel, 1)
        g.vector.memset(T.h[:, hw:E], 0.0).then_inc(s.hzero, 1)
    if not first:
        g.vector.memset(T.f[:], 1.0).then_inc(s.fone, 1)
        g.wait_ge(s.fone, 1)
        g.affine_select(T.f[:], T.f[:], [[1, 2], [-1, E]], AluOpType.is_equal, 0.0, 0, NB).then_inc(s.fsel, 1)
    if not last:
        g.vector.wait_ge(s.hzero, 1)
        g.vector.wait_ge(s.hsel, 1)
        g.vector.quantize_mx(T.hc[:, 0:W], T.hp[:, 0:W], T.h[:, 0:E]).then_inc(s.hq, 1)
        g.wait_ge(s.hq, 1)
        g.remote_dma(T.sc[:, 0:HEAD].bitcast(dt.uint8), T.hc[:, 0:HEAD].bitcast(dt.uint8), s.harr, s.hsent, pid, rid, mask)
        g.remote_dma(T.sp[:, 0:HEAD], T.hp[:, 0:HEAD], s.harr, s.hsent, pid, rid, mask)

    g.vector.wait_ge(s.vin, 16)
    g.vector.quantize_mx(T.vc[:, 0:W], T.vp[:, 0:W], T.vt[:, 0:E]).then_inc(s.vq, 1)
    g.vector.wait_ge(s.kin0, 16)
    g.tensor.wait_ge(s.vq, 1)
    for b in range(NB):
        if b == NB - 1:
            g.vector.wait_ge(s.kin1, 16)
        g.vector.quantize_mx(T.kc[:, cut(b)], T.kp[:, cut(b)], T.kt[:, cut(b, E)]).then_inc(s["kq%d" % b], 1)
        g.tensor.wait_ge(s["kq%d" % b], 1)
        g.tensor.matmul_mx(T.zb[:, bank(b)], T.kc[:, cut(b)], T.kp[:, cut(b)], T.vc[:, 0:W], T.vp[:, 0:W], True, True).then_inc(s["zm%d" % b], 1)

    if first:
        for b in range(NB - 1):
            g.scalar.wait_ge(s["zm%d" % b], 1)
            g.scalar.activation(T.tile[:, strip(b)], T.zb[:, bank(b)], copy, scale=C).then_inc(s.zsc, 1)
        b = NB - 1
        g.vector.wait_ge(s["zm%d" % b], 1)
        g.vector.tensor_scalar(T.tile[:, strip(b)], T.zb[:, bank(b)], C, None, AluOpType.mult).then_inc(s.til, 1)
        g.vector.wait_ge(s.zsc, NB - 1)
        g.vector.wait_ge(s.til, 1)
    else:
        g.vector.wait_ge(s.fsel, 1)
        g.vector.quantize_mx(T.sc[:, HEAD:2 * W], T.sp[:, HEAD:2 * W], T.f[:, hw:2 * E]).then_inc(s.sq, 1)
        for b in range(2, NB):
            g.vector.quantize_mx(T.sc[:, cut(b)], T.sp[:, cut(b)], T.f[:, E + 1 - b:2 * E + 1 - b]).then_inc(s.sq, 1)
        g.vector.wait_ge(s.qin, 16)
        g.vector.quantize_mx(T.qc[:, 0:W], T.qp[:, 0:W], T.qt[:, 0:E]).then_inc(s.qq, 1)
        for b in range(NB):
            g.scalar.wait_ge(s["zm%d" % b], 1)
            g.scalar.activation(T.zs[:, cut(b)], T.zb[:, bank(b)], copy, scale=C).then_inc(s.zsc, 1)
        g.tensor.wait_ge(s.sq, NB - 1)
        g.tensor.wait_ge(s.qq, 1)
        got = 2 * engines(T.cores[rank - 1], core)
        g.tensor.wait_ge(s.harr, got)
        g.tensor.wait_ge(s.arr, got)
        g.vector.wait_ge(s.zsc, NB)
        for b in range(NB):
            g.tensor.matmul_mx(T.db[:, bank(b)], T.sc[:, cut(b)], T.sp[:, cut(b)], T.rc[:, 0:W], T.rp[:, 0:W], True, True).then_inc(s["dm%d" % b], 1)
        pieces = [(0, 0, W // 2), (0, W // 2, W)] + [(b, 0, W) for b in range(1, NB)]
        for i, (b, lo, hi) in enumerate(pieces):
            if lo == 0:
                g.scalar.wait_ge(s["dm%d" % b], 1)
            c = slice(W * b + lo, W * b + hi)
            g.scalar.activation(T.ds[:, c], T.db[:, bank(b, lo, hi)], copy, scale=DEC).then_inc(s["dsc%d" % i], 1)
            g.vector.wait_ge(s["dsc%d" % i], 1)
            g.vector.tensor_tensor(T.tile[:, strip(b, lo, hi)], T.zs[:, c], T.ds[:, c], AluOpType.add).then_inc(s.til, 1)
        g.vector.wait_ge(s.til, len(pieces))

    g.vector.quantize_mx(T.tc[:, 0:W], T.tp[:, 0:W], T.tile[:, 0:E]).then_inc(s.st, 1)

    if not last:
        g.wait_ge(s.st, 1)
        g.remote_dma(T.rc[:, 0:W].bitcast(dt.uint8), T.tc[:, 0:W].bitcast(dt.uint8), s.arr, s.sent, pid, rid, mask)
        g.remote_dma(T.rp[:, 0:W], T.tp[:, 0:W], s.arr, s.sent, pid, rid, mask)
        g.wait_ge(s.hsent, 2 * engines(core, dst))
        g.sync.wait_ge(s.sent, 2 * engines(core, dst))
        if first:
            g.sync.dma_start(T.qt[:], T.q[:]).then_inc(s.qin, 16)
            g.vector.wait_ge(s.qin, 16)
            g.vector.quantize_mx(T.qc[:, 0:W], T.qp[:, 0:W], T.qt[:, 0:E]).then_inc(s.qq, 1)
            g.tensor.wait_ge(s.qq, 1)

    g.tensor.wait_ge(s.st, 1)
    g.tensor.matmul_mx(T.zb[:, bank(0)], T.tc[:, 0:W], T.tp[:, 0:W], T.qc[:, 0:W], T.qp[:, 0:W], True, True).then_inc(s.ymm, 1)
    g.vector.wait_ge(s.ymm, 1)
    g.vector.tensor_copy(T.ys[:], T.zb[:, bank(0)]).then_inc(s.ycp, 1)
    g.sync.wait_ge(s.ycp, 1)
    g.sync.dma_start(T.y[:], T.ys[:]).then_inc(s.yout, 16)
    g.sync.wait_ge(s.yout, 16)
